import numpy as np
import ml_dtypes


def mxq(x, axis, fmt="e4m3"):
    dtype, down = {"e4m3": (ml_dtypes.float8_e4m3fn, 7), "e5m2": (ml_dtypes.float8_e5m2, 14)}[fmt]
    v = np.moveaxis(np.asarray(x, np.float32).astype(ml_dtypes.bfloat16).astype(np.float64), axis, -1)
    blocks = v.reshape(v.shape[:-1] + (-1, 32))
    amax = np.abs(blocks).max(-1, keepdims=True)
    byte = np.maximum(np.where(amax > 0, np.frexp(amax)[1] - 1 + 127, 0) - down, 1)
    scale = np.exp2(byte - 127.0)
    codes = (blocks / scale).astype(np.float32).astype(dtype).astype(np.float64)
    return np.moveaxis((codes * scale).reshape(v.shape), -1, axis)


WIDE = False


def mx_kscale(k):
    if not WIDE:
        return np.ones(k)
    levels = np.array([10, -10, 5, -5, 0])
    if k % 512:
        return np.exp2(np.random.permutation(np.resize(levels, k // 32))).repeat(32)
    a = np.empty((k // 512, 16))
    for p in range(k // 512):
        a[p, :8] = np.random.permutation(np.resize(levels, 8))
        for g in range(8):
            far = levels[np.abs(levels - a[p, g]) >= 10]
            a[p, g + 8] = far[np.random.randint(len(far))]
    return np.exp2(a.ravel()).repeat(32)


def f64(x):
    return np.asarray(x).astype(np.float64)


E2M1 = np.array([0.0, 0.5, 1.0, 1.5, 2.0, 3.0, 4.0, 6.0, -0.0, -0.5, -1.0, -1.5, -2.0, -3.0, -4.0, -6.0])


def pack_weight(w, fmt):
    k, n = w.shape
    w = f64(np.asarray(w, np.float32).astype(ml_dtypes.bfloat16)).reshape(k // 32, 32, n)
    amax = np.abs(w).max(1)
    if fmt == "e4m3":
        byte = np.frexp(amax)[1] - 1 + 127 - 7
    else:
        mant, ex = np.frexp(amax / 6.0)
        byte = np.where(mant > 0.5, ex, ex - 1) + 127
    byte = np.clip(np.where(amax > 0, byte, 1), 1, 254)
    scaled = (w * np.exp2(127.0 - byte)[:, None, :]).reshape(k, n).astype(np.float32)
    by_word = np.ascontiguousarray(scaled.reshape(k // 512, 128, 4, n).transpose(0, 1, 3, 2))
    if fmt == "e4m3":
        words = by_word.astype(ml_dtypes.float8_e4m3fn).view(np.uint8)
    else:
        c = by_word.astype(ml_dtypes.float4_e2m1fn).view(np.uint8) & 0xF
        words = (c[..., 0::2] | (c[..., 1::2] << 4)).reshape(k // 512, 128, 2 * n)
    return np.ascontiguousarray(words), np.ascontiguousarray(byte.astype(np.uint8).reshape(k // 512, 16, n))


def unpack_weight(words, scales, fmt):
    g, _, n = scales.shape
    words = np.ascontiguousarray(words).reshape(g, 128, n, -1)
    if fmt == "e4m3":
        vals = words.view(ml_dtypes.float8_e4m3fn).astype(np.float64)
    else:
        nib = np.empty((g, 128, n, 4), np.uint8)
        nib[..., 0::2] = words & 0xF
        nib[..., 1::2] = words >> 4
        vals = E2M1[nib]
    vals = vals * np.repeat(np.exp2(scales.astype(np.float64) - 127.0), 8, axis=1)[..., None]
    return vals.transpose(0, 1, 3, 2).reshape(g * 512, n)


K, M, T = 1536, 1536, 512


def setup_inputs():
    n = np.random.standard_normal
    s = mx_kscale(K)[:, None]
    p_wr = pack_weight(n((K, M)) / np.sqrt(2 * K) / s, "e4m3")
    p_wi = pack_weight(n((K, M)) / np.sqrt(2 * K) / s, "e2m1")
    return {
        "xr": (n((K, T)) * s).astype(np.float32),
        "xi": (n((K, T)) * s).astype(np.float32),
        "wr_words": p_wr[0],
        "wr_scales": p_wr[1],
        "wi_words": p_wi[0],
        "wi_scales": p_wi[1],
    }


def reference(xr, xi, wr_words, wr_scales, wi_words, wi_scales):
    xr_ = mxq(f64(xr), 0, "e4m3")
    xi_ = mxq(f64(xi), 0, "e4m3")
    wr_ = unpack_weight(wr_words, wr_scales, "e4m3")
    wi_ = unpack_weight(wi_words, wi_scales, "e2m1")
    return wr_.T @ xr_ - wi_.T @ xi_, wr_.T @ xi_ + wi_.T @ xr_

@@ -1,0 +1,267 @@
+from contextlib import ExitStack
+
+import concourse.mybir as mybir
+
+K, M, T = 1536, 1536, 512
+FLOPS = 4 * 2 * K * M * T
+
+F32 = mybir.dt.float32
+BF16 = mybir.dt.bfloat16
+I32 = mybir.dt.int32
+U32 = mybir.dt.uint32
+U8 = mybir.dt.uint8
+FP8X4 = mybir.dt.float8_e4m3fn_x4
+FP4X4 = mybir.dt.float4_e2m1fn_x4
+ALU = mybir.AluOpType
+ACT = mybir.ActivationFunctionType
+
+P = 128
+PACK = 4
+K_PASS = P * PACK
+PASSES = K // K_PASS
+N_TILES = M // P
+BANKS = 8
+HALF = T // 2
+WR_SCALE_ROW = 4
+NEIGHBOURS = 2
+
+FIRST = range(0, 4)
+SECOND = range(4, 6)
+HELD = range(6, 10)
+LAST = range(10, 12)
+VECTOR_SHARE = 5
+RESULT_BUFS = 12
+
+
+def tile_mix_cplx_fm_none_kernel(tc, xr, xi, wr_words, wr_scales, wi_words, wi_scales, out_0, out_1):
+    nc = tc.nc
+    outs = (out_0, out_1)
+    x_in = {"xr": xr, "xi": xi}
+
+    with ExitStack() as ctx:
+        keep = ctx.enter_context(tc.tile_pool(name="keep", bufs=1))
+        results = ctx.enter_context(tc.tile_pool(name="results", bufs=RESULT_BUFS))
+        psum = ctx.enter_context(tc.psum_pool(name="psum", bufs=1))
+        ctx.enter_context(tc.manual_schedule())
+
+        raw = {}
+        wr_codes, wi_codes, wr_scale, wi_scale = {}, {}, {}, {}
+
+        def load_x(name, a, t0, t1):
+            rows = keep.tile([P, PACK, t1 - t0], F32, name="raw_%s_%d_%d" % (name, a, t0))
+            src = x_in[name][a * K_PASS : (a + 1) * K_PASS, t0:t1]
+            nc.sync.dma_start(out=rows[:], in_=src.rearrange("(p j) w -> p j w", j=PACK))
+            raw[(name, a, t0)] = rows
+
+        def load_wr(passes, tiles):
+            c0, c1 = tiles.start * P, tiles.stop * P
+            words = keep.tile([P, len(passes), c1 - c0], U32, align_bytes=64, name="wr_%d_%d" % (passes.start, c0))
+            src = wr_words[passes.start : passes.stop].rearrange("a p n i -> p a (n i)")
+            nc.sync.dma_start(out=words[:].bitcast(I32), in_=src[:, :, PACK * c0 : PACK * c1].bitcast(I32))
+            for a in passes:
+                for n in tiles:
+                    lo = n * P - c0
+                    wr_codes[(a, n)] = words[:, a - passes.start, lo : lo + P]
+
+        def load_wi(passes, tiles):
+            c0, c1 = tiles.start * P, tiles.stop * P
+            words = keep.tile([P, len(passes), 2 * (c1 - c0)], U8, align_bytes=64, name="wi_%d_%d" % (passes.start, c0))
+            src = wi_words[passes.start : passes.stop].rearrange("a p b -> p a b")
+            nc.sync.dma_start(out=words[:].bitcast(I32), in_=src[:, :, 2 * c0 : 2 * c1].bitcast(I32))
+            for a in passes:
+                for n in tiles:
+                    lo = 2 * (n * P - c0)
+                    wi_codes[(a, n)] = words[:, a - passes.start, lo : lo + 2 * P]
+
+        def new_plane(passes):
+            plane = keep.tile([P, len(passes), M], U8, align_bytes=64, name="plane_%d" % passes.start)
+            nc.vector.memset(plane[:].bitcast(I32), 0)
+            for a in passes:
+                for n in range(N_TILES):
+                    wi_scale[(a, n)] = plane[:, a - passes.start, n * P : (n + 1) * P]
+                    wr_scale[(a, n)] = plane[WR_SCALE_ROW:, a - passes.start, n * P : (n + 1) * P]
+            return plane
+
+        def load_scales(plane, scales, passes, first_row):
+            src = scales[passes.start : passes.stop].rearrange("a (q r) n -> r q a n", r=4)
+            for r in range(4):
+                nc.sync.dma_start(out=plane[first_row + r : P : 32, :, :].bitcast(I32), in_=src[r].bitcast(I32))
+
+        pass0, later = range(0, 1), range(1, PASSES)
+        plane0 = new_plane(pass0)
+        plane12 = new_plane(later)
+
+        load_x("xi", 0, 0, HALF)
+        load_scales(plane0, wr_scales, pass0, WR_SCALE_ROW)
+        load_wr(pass0, FIRST)
+        load_x("xi", 0, HALF, T)
+        load_wi(pass0, FIRST)
+        load_scales(plane0, wi_scales, pass0, 0)
+        load_x("xr", 0, 0, HALF)
+        load_x("xr", 0, HALF, T)
+        early = range(SECOND.start, HELD.stop)
+        load_wr(pass0, early)
+        load_wi(pass0, early)
+        load_scales(plane12, wr_scales, later, WR_SCALE_ROW)
+        load_scales(plane12, wi_scales, later, 0)
+        for a in later:
+            load_x("xi", a, 0, T)
+            load_wr(range(a, a + 1), HELD)
+            load_wi(range(a, a + 1), HELD)
+            load_x("xr", a, 0, T)
+        for tiles in (FIRST, SECOND):
+            load_wr(later, tiles)
+            load_wi(later, tiles)
+        load_wr(range(PASSES), LAST)
+        load_wi(range(PASSES), LAST)
+
+        x_codes, x_scale, grouped = {}, {}, {}
+        for name in ("xr", "xi", "xn"):
+            for a in range(PASSES):
+                x_codes[(name, a)] = keep.tile([P, T], U32, align_bytes=64, name="codes_%s_%d" % (name, a))
+                x_scale[(name, a)] = keep.tile([P, T], U8, align_bytes=64, name="scale_%s_%d" % (name, a))
+
+        def interleave_views(name, source, a, t0, c0, c1):
+            rows = raw[(source, a, t0)]
+            if (name, a, t0) not in grouped:
+                grouped[(name, a, t0)] = keep.tile(
+                    [P, rows.shape[2], PACK], BF16, align_bytes=64, name="grouped_%s_%d_%d" % (name, a, t0)
+                )
+            dst = grouped[(name, a, t0)][:, c0:c1, :].rearrange("p (c i) j -> p c j i", i=NEIGHBOURS)
+            src = rows[:, :, c0:c1].rearrange("p j (c i) -> p c j i", i=NEIGHBOURS)
+            return dst, src
+
+        def cast_vector(name, a, t0):
+            dst, src = interleave_views(name, name, a, t0, 0, raw[(name, a, t0)].shape[2])
+            nc.vector.tensor_copy(out=dst, in_=src)
+
+        def cast_shared(name, a, t0):
+            width = raw[(name, a, t0)].shape[2]
+            cut = width * VECTOR_SHARE // 8
+            dst, src = interleave_views(name, name, a, t0, 0, cut)
+            nc.vector.tensor_copy(out=dst, in_=src)
+            dst, src = interleave_views(name, name, a, t0, cut, width)
+            nc.scalar.copy(out=dst, in_=src)
+
+        def negate_scalar(a, t0):
+            dst, src = interleave_views("xn", "xi", a, t0, 0, raw[("xi", a, t0)].shape[2])
+            nc.scalar.activation(out=dst, in_=src, func=ACT.Copy, scale=-1.0)
+
+        def negate_vector(a):
+            grouped[("xn", a, 0)] = keep.tile([P, T, PACK], BF16, align_bytes=64, name="grouped_xn_%d" % a)
+            nc.vector.tensor_scalar(
+                out=grouped[("xn", a, 0)][:], in0=grouped[("xi", a, 0)][:], scalar1=-1.0, scalar2=None, op0=ALU.mult
+            )
+
+        def quantise(name, a, t0):
+            source = grouped[(name, a, t0)]
+            t1 = t0 + source.shape[1]
+            nc.vector.quantize_mx(
+                out=x_codes[(name, a)][:, t0:t1].bitcast(FP8X4),
+                scales=x_scale[(name, a)][:, t0:t1],
+                in_=source[:].rearrange("p w j -> p (w j)"),
+            )
+
+        acc, partial = {}, {}
+        opened = []
+
+        def mm(weight, name, a, n, o, t0=0, t1=T, stop=False, bank=None):
+            start = (n, o) not in acc
+            if start:
+                if bank is None:
+                    bank = len(opened) % BANKS
+                opened.append((n, o))
+                acc[(n, o)] = psum.tile([P, T], F32, name="bank%d" % bank)
+            if weight == "wr":
+                codes, scale = wr_codes[(a, n)].bitcast(FP8X4), wr_scale[(a, n)]
+            else:
+                codes, scale = wi_codes[(a, n)].bitcast(FP4X4), wi_scale[(a, n)]
+            nc.tensor.matmul_mx(
+                out=acc[(n, o)][:, t0:t1],
+                lhsT=codes,
+                lhsT_scale=scale,
+                rhs=x_codes[(name, a)][:, t0:t1].bitcast(FP8X4),
+                rhs_scale=x_scale[(name, a)][:, t0:t1],
+                start=start,
+                stop=stop,
+            )
+
+        def park(n, o):
+            partial[(n, o)] = keep.tile([P, T], F32, name="partial_%d_%d" % (n, o))
+            nc.scalar.copy(out=partial[(n, o)][:], in_=acc.pop((n, o))[:])
+
+        def finish(n, o, on_vector, pieces=1):
+            bank = acc.pop((n, o))
+            result = results.tile([P, T], F32, name="result")
+            step = T // pieces
+            for t0 in range(0, T, step):
+                cols = slice(t0, t0 + step)
+                if (n, o) in partial:
+                    nc.vector.tensor_tensor(
+                        out=result[:, cols], in0=bank[:, cols], in1=partial[(n, o)][:, cols], op=ALU.add
+                    )
+                elif on_vector:
+                    nc.vector.tensor_copy(out=result[:, cols], in_=bank[:, cols])
+                else:
+                    nc.scalar.copy(out=result[:, cols], in_=bank[:, cols])
+                nc.sync.dma_start(out=outs[o][n * P : (n + 1) * P, cols], in_=result[:, cols])
+
+        terms = ((("wi", "xn"), ("wr", "xr")), (("wr", "xi"), ("wi", "xr")))
+
+        for t0 in (0, HALF):
+            cast_vector("xi", 0, t0)
+            negate_scalar(0, t0)
+            quantise("xi", 0, t0)
+            quantise("xn", 0, t0)
+        for t0 in (0, HALF):
+            cast_shared("xr", 0, t0)
+            quantise("xr", 0, t0)
+
+        for t0 in (0, HALF):
+            for n in FIRST:
+                mm("wr", "xi", 0, n, 1, t0, t0 + HALF, bank=2 * n + 1)
+        for n in FIRST:
+            mm("wi", "xn", 0, n, 0, bank=2 * n)
+        for n in FIRST:
+            mm("wr", "xr", 0, n, 0, 0, HALF)
+        for n in FIRST:
+            mm("wr", "xr", 0, n, 0, HALF, T, stop=True)
+            park(n, 0)
+            mm("wi", "xr", 0, n, 1, stop=True)
+            park(n, 1)
+
+        for n in SECOND:
+            for o in (0, 1):
+                mm(*terms[o][0], 0, n, o)
+                mm(*terms[o][1], 0, n, o, stop=True)
+                park(n, o)
+        for n in HELD:
+            for o in (0, 1):
+                mm(*terms[o][0], 0, n, o)
+                mm(*terms[o][1], 0, n, o)
+
+        for a in later:
+            final = a == PASSES - 1
+            cast_vector("xi", a, 0)
+            negate_vector(a)
+            quantise("xi", a, 0)
+            quantise("xn", a, 0)
+            cast_shared("xr", a, 0)
+            quantise("xr", a, 0)
+            for o in (1, 0):
+                for n in HELD:
+                    mm(*terms[o][0], a, n, o)
+            for n in HELD:
+                for o in (0, 1):
+                    mm(*terms[o][1], a, n, o, stop=final)
+                    if final:
+                        finish(n, o, on_vector=(o == 1))
+
+        for n in list(FIRST) + list(SECOND) + list(LAST):
+            passes = range(PASSES) if n in LAST else later
+            for o in (0, 1):
+                steps = [(w, x, a) for a in passes for (w, x) in terms[o]]
+                for s, (w, x, a) in enumerate(steps):
+                    mm(w, x, a, n, o, stop=(s == len(steps) - 1))
+                very_last = n == LAST.stop - 1 and o == 1
+                finish(n, o, on_vector=(o == 1), pieces=2 if very_last else 1)

@@ -26,11 +26,10 @@ WR_SCALE_ROW = 4
 NEIGHBOURS = 2
 
 FIRST = range(0, 4)
-SECOND = range(4, 6)
-HELD = range(6, 10)
-LAST = range(10, 12)
+SECOND = range(4, 8)
+HELD = range(8, 12)
 VECTOR_SHARE = 5
-RESULT_BUFS = 12
+RESULT_BUFS = 10
 
 
 def tile_mix_cplx_fm_none_kernel(tc, xr, xi, wr_words, wr_scales, wi_words, wi_scales, out_0, out_1):
@@ -73,47 +72,52 @@ def tile_mix_cplx_fm_none_kernel(tc, xr, xi, wr_words, wr_scales, wi_words, wi_s
                     lo = 2 * (n * P - c0)
                     wi_codes[(a, n)] = words[:, a - passes.start, lo : lo + 2 * P]
 
-        def new_plane(passes):
-            plane = keep.tile([P, len(passes), M], U8, align_bytes=64, name="plane_%d" % passes.start)
+        def new_plane(name, passes, tiles):
+            plane = keep.tile([P, len(passes), len(tiles) * P], U8, align_bytes=64, name=name)
             nc.vector.memset(plane[:].bitcast(I32), 0)
-            for a in passes:
-                for n in range(N_TILES):
-                    wi_scale[(a, n)] = plane[:, a - passes.start, n * P : (n + 1) * P]
-                    wr_scale[(a, n)] = plane[WR_SCALE_ROW:, a - passes.start, n * P : (n + 1) * P]
             return plane
 
-        def load_scales(plane, scales, passes, first_row):
-            src = scales[passes.start : passes.stop].rearrange("a (q r) n -> r q a n", r=4)
+        def load_scales(plane, scales, views, passes, tiles, first_row):
+            src = scales[passes.start : passes.stop, :, tiles.start * P : tiles.stop * P]
+            src = src.rearrange("a (q r) n -> r q a n", r=4)
             for r in range(4):
                 nc.sync.dma_start(out=plane[first_row + r : P : 32, :, :].bitcast(I32), in_=src[r].bitcast(I32))
+            for a in passes:
+                for n in tiles:
+                    lo = (n - tiles.start) * P
+                    views[(a, n)] = plane[first_row:, a - passes.start, lo : lo + P]
 
         pass0, later = range(0, 1), range(1, PASSES)
-        plane0 = new_plane(pass0)
-        plane12 = new_plane(later)
+        others, every = range(FIRST.stop, N_TILES), range(N_TILES)
+        plane_wr_first = new_plane("plane_wr_first", pass0, FIRST)
+        plane_wi_first = new_plane("plane_wi_first", pass0, FIRST)
+        plane_others = new_plane("plane_others", pass0, others)
+        plane_later = new_plane("plane_later", later, every)
 
         load_x("xi", 0, 0, HALF)
-        load_scales(plane0, wr_scales, pass0, WR_SCALE_ROW)
+        load_scales(plane_wr_first, wr_scales, wr_scale, pass0, FIRST, WR_SCALE_ROW)
         load_wr(pass0, FIRST)
         load_x("xi", 0, HALF, T)
         load_wi(pass0, FIRST)
-        load_scales(plane0, wi_scales, pass0, 0)
+        load_scales(plane_wi_first, wi_scales, wi_scale, pass0, FIRST, 0)
         load_x("xr", 0, 0, HALF)
         load_x("xr", 0, HALF, T)
-        early = range(SECOND.start, HELD.stop)
-        load_wr(pass0, early)
-        load_wi(pass0, early)
-        load_scales(plane12, wr_scales, later, WR_SCALE_ROW)
-        load_scales(plane12, wi_scales, later, 0)
+        load_scales(plane_others, wi_scales, wi_scale, pass0, others, 0)
+        load_wi(pass0, others)
+        load_wr(pass0, others)
+        load_scales(plane_others, wr_scales, wr_scale, pass0, others, WR_SCALE_ROW)
         for a in later:
             load_x("xi", a, 0, T)
             load_wr(range(a, a + 1), HELD)
+            if a == 1:
+                load_scales(plane_later, wr_scales, wr_scale, later, every, WR_SCALE_ROW)
             load_wi(range(a, a + 1), HELD)
             load_x("xr", a, 0, T)
+            if a == 1:
+                load_scales(plane_later, wi_scales, wi_scale, later, every, 0)
         for tiles in (FIRST, SECOND):
             load_wr(later, tiles)
             load_wi(later, tiles)
-        load_wr(range(PASSES), LAST)
-        load_wi(range(PASSES), LAST)
 
         x_codes, x_scale, grouped = {}, {}, {}
         for name in ("xr", "xi", "xn"):
@@ -186,9 +190,12 @@ def tile_mix_cplx_fm_none_kernel(tc, xr, xi, wr_words, wr_scales, wi_words, wi_s
                 stop=stop,
             )
 
-        def park(n, o):
+        def park(n, o, on_vector=False):
             partial[(n, o)] = keep.tile([P, T], F32, name="partial_%d_%d" % (n, o))
-            nc.scalar.copy(out=partial[(n, o)][:], in_=acc.pop((n, o))[:])
+            if on_vector:
+                nc.vector.tensor_copy(out=partial[(n, o)][:], in_=acc.pop((n, o))[:])
+            else:
+                nc.scalar.copy(out=partial[(n, o)][:], in_=acc.pop((n, o))[:])
 
         def finish(n, o, on_vector, pieces=1):
             bank = acc.pop((n, o))
@@ -228,7 +235,7 @@ def tile_mix_cplx_fm_none_kernel(tc, xr, xi, wr_words, wr_scales, wi_words, wi_s
             mm("wr", "xr", 0, n, 0, HALF, T, stop=True)
             park(n, 0)
             mm("wi", "xr", 0, n, 1, stop=True)
-            park(n, 1)
+            park(n, 1, on_vector=True)
 
         for n in SECOND:
             for o in (0, 1):
@@ -257,11 +264,10 @@ def tile_mix_cplx_fm_none_kernel(tc, xr, xi, wr_words, wr_scales, wi_words, wi_s
                     if final:
                         finish(n, o, on_vector=(o == 1))
 
-        for n in list(FIRST) + list(SECOND) + list(LAST):
-            passes = range(PASSES) if n in LAST else later
+        for n in range(FIRST.start, SECOND.stop):
             for o in (0, 1):
-                steps = [(w, x, a) for a in passes for (w, x) in terms[o]]
+                steps = [(w, x, a) for a in later for (w, x) in terms[o]]
                 for s, (w, x, a) in enumerate(steps):
                     mm(w, x, a, n, o, stop=(s == len(steps) - 1))
-                very_last = n == LAST.stop - 1 and o == 1
+                very_last = n == SECOND.stop - 1 and o == 1
                 finish(n, o, on_vector=(o == 1), pieces=2 if very_last else 1)

@@ -19,23 +19,36 @@ P = 128
 PACK = 4
 K_PASS = P * PACK
 PASSES = K // K_PASS
-N_TILES = M // P
 BANKS = 8
 HALF = T // 2
-WR_SCALE_ROW = 4
-NEIGHBOURS = 2
+QUARTER = T // 4
+MX_ALIGN = 64
+QUADRANT = 32
+SCALE_ROWS = 4
+
+FIRST_SCALE_ROW = {"wi": 0, "wr": SCALE_ROWS}
+WORD_BYTES = {"wi": 2, "wr": 4}
 
 FIRST = range(0, 4)
 SECOND = range(4, 8)
 HELD = range(8, 12)
-VECTOR_SHARE = 5
+
+TERMS = ((("wi", "xn"), ("wr", "xr")), (("wr", "xi"), ("wi", "xr")))
+
+NEIGHBOURS = 2
+VECTOR_EIGHTHS = 5
 RESULT_BUFS = 10
 
 
 def tile_mix_cplx_fm_none_kernel(tc, xr, xi, wr_words, wr_scales, wi_words, wi_scales, out_0, out_1):
     nc = tc.nc
     outs = (out_0, out_1)
-    x_in = {"xr": xr, "xi": xi}
+    x_hbm = {"xr": xr, "xi": xi}
+    words_hbm = {"wr": wr_words.rearrange("a p n j -> p a (n j)"), "wi": wi_words.rearrange("a p b -> p a b")}
+    scales_hbm = {"wr": wr_scales, "wi": wi_scales}
+
+    pass0, later = range(0, 1), range(1, PASSES)
+    after_first, parked = range(SECOND.start, HELD.stop), range(FIRST.start, SECOND.stop)
 
     with ExitStack() as ctx:
         keep = ctx.enter_context(tc.tile_pool(name="keep", bufs=1))
@@ -44,118 +57,118 @@ def tile_mix_cplx_fm_none_kernel(tc, xr, xi, wr_words, wr_scales, wi_words, wi_s
         ctx.enter_context(tc.manual_schedule())
 
         raw = {}
-        wr_codes, wi_codes, wr_scale, wi_scale = {}, {}, {}, {}
+        w_codes, w_scale = {}, {}
 
         def load_x(name, a, t0, t1):
             rows = keep.tile([P, PACK, t1 - t0], F32, name="raw_%s_%d_%d" % (name, a, t0))
-            src = x_in[name][a * K_PASS : (a + 1) * K_PASS, t0:t1]
+            src = x_hbm[name][a * K_PASS : (a + 1) * K_PASS, t0:t1]
             nc.sync.dma_start(out=rows[:], in_=src.rearrange("(p j) w -> p j w", j=PACK))
             raw[(name, a, t0)] = rows
 
-        def load_wr(passes, tiles):
-            c0, c1 = tiles.start * P, tiles.stop * P
-            words = keep.tile([P, len(passes), c1 - c0], U32, align_bytes=64, name="wr_%d_%d" % (passes.start, c0))
-            src = wr_words[passes.start : passes.stop].rearrange("a p n i -> p a (n i)")
-            nc.sync.dma_start(out=words[:].bitcast(I32), in_=src[:, :, PACK * c0 : PACK * c1].bitcast(I32))
+        def load_words(weight, passes, tiles):
+            tile_bytes = P * WORD_BYTES[weight]
+            words = keep.tile(
+                [P, len(passes), len(tiles) * tile_bytes],
+                U8,
+                align_bytes=MX_ALIGN,
+                name="words_%s_%d_%d" % (weight, passes.start, tiles.start),
+            )
+            src = words_hbm[weight][:, passes.start : passes.stop, tiles.start * tile_bytes : tiles.stop * tile_bytes]
+            nc.sync.dma_start(out=words[:].bitcast(I32), in_=src.bitcast(I32))
             for a in passes:
                 for n in tiles:
-                    lo = n * P - c0
-                    wr_codes[(a, n)] = words[:, a - passes.start, lo : lo + P]
-
-        def load_wi(passes, tiles):
-            c0, c1 = tiles.start * P, tiles.stop * P
-            words = keep.tile([P, len(passes), 2 * (c1 - c0)], U8, align_bytes=64, name="wi_%d_%d" % (passes.start, c0))
-            src = wi_words[passes.start : passes.stop].rearrange("a p b -> p a b")
-            nc.sync.dma_start(out=words[:].bitcast(I32), in_=src[:, :, 2 * c0 : 2 * c1].bitcast(I32))
-            for a in passes:
-                for n in tiles:
-                    lo = 2 * (n * P - c0)
-                    wi_codes[(a, n)] = words[:, a - passes.start, lo : lo + 2 * P]
+                    lo = (n - tiles.start) * tile_bytes
+                    w_codes[(weight, a, n)] = words[:, a - passes.start, lo : lo + tile_bytes]
 
         def new_plane(name, passes, tiles):
-            plane = keep.tile([P, len(passes), len(tiles) * P], U8, align_bytes=64, name=name)
+            plane = keep.tile([P, len(passes), len(tiles) * P], U8, align_bytes=MX_ALIGN, name=name)
             nc.vector.memset(plane[:].bitcast(I32), 0)
             return plane
 
-        def load_scales(plane, scales, views, passes, tiles, first_row):
-            src = scales[passes.start : passes.stop, :, tiles.start * P : tiles.stop * P]
-            src = src.rearrange("a (q r) n -> r q a n", r=4)
-            for r in range(4):
-                nc.sync.dma_start(out=plane[first_row + r : P : 32, :, :].bitcast(I32), in_=src[r].bitcast(I32))
+        def load_scales(plane, weight, passes, tiles):
+            first_row = FIRST_SCALE_ROW[weight]
+            src = scales_hbm[weight][passes.start : passes.stop, :, tiles.start * P : tiles.stop * P]
+            src = src.rearrange("a (q r) n -> r q a n", r=SCALE_ROWS)
+            for r in range(SCALE_ROWS):
+                nc.sync.dma_start(out=plane[first_row + r : P : QUADRANT, :, :].bitcast(I32), in_=src[r].bitcast(I32))
             for a in passes:
                 for n in tiles:
                     lo = (n - tiles.start) * P
-                    views[(a, n)] = plane[first_row:, a - passes.start, lo : lo + P]
+                    w_scale[(weight, a, n)] = plane[first_row:, a - passes.start, lo : lo + P]
 
-        pass0, later = range(0, 1), range(1, PASSES)
-        others, every = range(FIRST.stop, N_TILES), range(N_TILES)
         plane_wr_first = new_plane("plane_wr_first", pass0, FIRST)
         plane_wi_first = new_plane("plane_wi_first", pass0, FIRST)
-        plane_others = new_plane("plane_others", pass0, others)
-        plane_later = new_plane("plane_later", later, every)
+        plane_after_first = new_plane("plane_after_first", pass0, after_first)
+        plane_held = new_plane("plane_held", later, HELD)
+        plane_parked = new_plane("plane_parked", later, parked)
 
         load_x("xi", 0, 0, HALF)
-        load_scales(plane_wr_first, wr_scales, wr_scale, pass0, FIRST, WR_SCALE_ROW)
-        load_wr(pass0, FIRST)
+        load_scales(plane_wr_first, "wr", pass0, FIRST)
+        load_words("wr", pass0, FIRST)
         load_x("xi", 0, HALF, T)
-        load_wi(pass0, FIRST)
-        load_scales(plane_wi_first, wi_scales, wi_scale, pass0, FIRST, 0)
+        load_words("wi", pass0, FIRST)
+        load_scales(plane_wi_first, "wi", pass0, FIRST)
         load_x("xr", 0, 0, HALF)
         load_x("xr", 0, HALF, T)
-        load_scales(plane_others, wi_scales, wi_scale, pass0, others, 0)
-        load_wi(pass0, others)
-        load_wr(pass0, others)
-        load_scales(plane_others, wr_scales, wr_scale, pass0, others, WR_SCALE_ROW)
+        load_scales(plane_after_first, "wi", pass0, after_first)
+        load_words("wi", pass0, SECOND)
+        load_words("wr", pass0, SECOND)
+        load_scales(plane_after_first, "wr", pass0, after_first)
+        load_words("wi", pass0, HELD)
+        load_words("wr", pass0, HELD)
         for a in later:
             load_x("xi", a, 0, T)
-            load_wr(range(a, a + 1), HELD)
-            if a == 1:
-                load_scales(plane_later, wr_scales, wr_scale, later, every, WR_SCALE_ROW)
-            load_wi(range(a, a + 1), HELD)
+            load_words("wr", range(a, a + 1), HELD)
+            if a == later.start:
+                load_scales(plane_held, "wr", later, HELD)
+            load_words("wi", range(a, a + 1), HELD)
             load_x("xr", a, 0, T)
-            if a == 1:
-                load_scales(plane_later, wi_scales, wi_scale, later, every, 0)
-        for tiles in (FIRST, SECOND):
-            load_wr(later, tiles)
-            load_wi(later, tiles)
+            if a == later.start:
+                load_scales(plane_held, "wi", later, HELD)
+        load_scales(plane_parked, "wi", later, parked)
+        load_words("wi", later, FIRST)
+        load_words("wr", later, FIRST)
+        load_scales(plane_parked, "wr", later, parked)
+        load_words("wi", later, SECOND)
+        load_words("wr", later, SECOND)
 
-        x_codes, x_scale, grouped = {}, {}, {}
+        x_codes, x_scale = {}, {}
         for name in ("xr", "xi", "xn"):
             for a in range(PASSES):
-                x_codes[(name, a)] = keep.tile([P, T], U32, align_bytes=64, name="codes_%s_%d" % (name, a))
-                x_scale[(name, a)] = keep.tile([P, T], U8, align_bytes=64, name="scale_%s_%d" % (name, a))
+                x_codes[(name, a)] = keep.tile([P, T], U32, align_bytes=MX_ALIGN, name="codes_%s_%d" % (name, a))
+                x_scale[(name, a)] = keep.tile([P, T], U8, align_bytes=MX_ALIGN, name="scale_%s_%d" % (name, a))
+
+        grouped = {}
+
+        def new_grouped(name, source, a, t0):
+            width = raw[(source, a, t0)].shape[2]
+            grouped[(name, a, t0)] = keep.tile(
+                [P, width, PACK], BF16, align_bytes=MX_ALIGN, name="grouped_%s_%d_%d" % (name, a, t0)
+            )
+            return width
 
         def interleave_views(name, source, a, t0, c0, c1):
-            rows = raw[(source, a, t0)]
-            if (name, a, t0) not in grouped:
-                grouped[(name, a, t0)] = keep.tile(
-                    [P, rows.shape[2], PACK], BF16, align_bytes=64, name="grouped_%s_%d_%d" % (name, a, t0)
-                )
             dst = grouped[(name, a, t0)][:, c0:c1, :].rearrange("p (c i) j -> p c j i", i=NEIGHBOURS)
-            src = rows[:, :, c0:c1].rearrange("p j (c i) -> p c j i", i=NEIGHBOURS)
+            src = raw[(source, a, t0)][:, :, c0:c1].rearrange("p j (c i) -> p c j i", i=NEIGHBOURS)
             return dst, src
 
-        def cast_vector(name, a, t0):
-            dst, src = interleave_views(name, name, a, t0, 0, raw[(name, a, t0)].shape[2])
+        def round_on_vector(name, a, t0):
+            width = new_grouped(name, name, a, t0)
+            dst, src = interleave_views(name, name, a, t0, 0, width)
             nc.vector.tensor_copy(out=dst, in_=src)
 
-        def cast_shared(name, a, t0):
-            width = raw[(name, a, t0)].shape[2]
-            cut = width * VECTOR_SHARE // 8
+        def round_on_both(name, a, t0):
+            width = new_grouped(name, name, a, t0)
+            cut = width * VECTOR_EIGHTHS // 8
             dst, src = interleave_views(name, name, a, t0, 0, cut)
             nc.vector.tensor_copy(out=dst, in_=src)
             dst, src = interleave_views(name, name, a, t0, cut, width)
             nc.scalar.copy(out=dst, in_=src)
 
-        def negate_scalar(a, t0):
-            dst, src = interleave_views("xn", "xi", a, t0, 0, raw[("xi", a, t0)].shape[2])
+        def negate_on_scalar(a, t0):
+            width = new_grouped("xn", "xi", a, t0)
+            dst, src = interleave_views("xn", "xi", a, t0, 0, width)
             nc.scalar.activation(out=dst, in_=src, func=ACT.Copy, scale=-1.0)
-
-        def negate_vector(a):
-            grouped[("xn", a, 0)] = keep.tile([P, T, PACK], BF16, align_bytes=64, name="grouped_xn_%d" % a)
-            nc.vector.tensor_scalar(
-                out=grouped[("xn", a, 0)][:], in0=grouped[("xi", a, 0)][:], scalar1=-1.0, scalar2=None, op0=ALU.mult
-            )
 
         def quantise(name, a, t0):
             source = grouped[(name, a, t0)]
@@ -166,108 +179,113 @@ def tile_mix_cplx_fm_none_kernel(tc, xr, xi, wr_words, wr_scales, wi_words, wi_s
                 in_=source[:].rearrange("p w j -> p (w j)"),
             )
 
-        acc, partial = {}, {}
+        open_sums = {}
+        partial = {}
         opened = []
 
-        def mm(weight, name, a, n, o, t0=0, t1=T, stop=False, bank=None):
-            start = (n, o) not in acc
+        def multiply(term, a, n, o, t0=0, t1=T, stop=False, bank=None):
+            weight, name = term
+            start = (n, o) not in open_sums
             if start:
                 if bank is None:
                     bank = len(opened) % BANKS
                 opened.append((n, o))
-                acc[(n, o)] = psum.tile([P, T], F32, name="bank%d" % bank)
-            if weight == "wr":
-                codes, scale = wr_codes[(a, n)].bitcast(FP8X4), wr_scale[(a, n)]
-            else:
-                codes, scale = wi_codes[(a, n)].bitcast(FP4X4), wi_scale[(a, n)]
+                open_sums[(n, o)] = psum.tile([P, T], F32, name="bank%d" % bank)
             nc.tensor.matmul_mx(
-                out=acc[(n, o)][:, t0:t1],
-                lhsT=codes,
-                lhsT_scale=scale,
+                out=open_sums[(n, o)][:, t0:t1],
+                lhsT=w_codes[(weight, a, n)].bitcast(FP8X4 if weight == "wr" else FP4X4),
+                lhsT_scale=w_scale[(weight, a, n)],
                 rhs=x_codes[(name, a)][:, t0:t1].bitcast(FP8X4),
                 rhs_scale=x_scale[(name, a)][:, t0:t1],
                 start=start,
                 stop=stop,
             )
 
-        def park(n, o, on_vector=False):
-            partial[(n, o)] = keep.tile([P, T], F32, name="partial_%d_%d" % (n, o))
+        def multiply_half(term, a, n, o, t0, stop=False, bank=None):
+            width = HALF if term[0] == "wr" else QUARTER
+            for lo in range(t0, t0 + HALF, width):
+                multiply(term, a, n, o, lo, lo + width, stop=stop and lo + width == t0 + HALF, bank=bank)
+
+        def copy_out(dst, src, on_vector):
             if on_vector:
-                nc.vector.tensor_copy(out=partial[(n, o)][:], in_=acc.pop((n, o))[:])
+                nc.vector.tensor_copy(out=dst, in_=src)
             else:
-                nc.scalar.copy(out=partial[(n, o)][:], in_=acc.pop((n, o))[:])
+                nc.scalar.copy(out=dst, in_=src)
 
-        def finish(n, o, on_vector, pieces=1):
-            bank = acc.pop((n, o))
+        def park(n, o, on_vector):
+            partial[(n, o)] = keep.tile([P, T], F32, name="partial_%d_%d" % (n, o))
+            copy_out(partial[(n, o)][:], open_sums.pop((n, o))[:], on_vector)
+
+        def finish(n, o, t0=0, t1=T):
+            total = open_sums.pop((n, o))[:, t0:t1]
             result = results.tile([P, T], F32, name="result")
-            step = T // pieces
-            for t0 in range(0, T, step):
-                cols = slice(t0, t0 + step)
-                if (n, o) in partial:
-                    nc.vector.tensor_tensor(
-                        out=result[:, cols], in0=bank[:, cols], in1=partial[(n, o)][:, cols], op=ALU.add
-                    )
-                elif on_vector:
-                    nc.vector.tensor_copy(out=result[:, cols], in_=bank[:, cols])
-                else:
-                    nc.scalar.copy(out=result[:, cols], in_=bank[:, cols])
-                nc.sync.dma_start(out=outs[o][n * P : (n + 1) * P, cols], in_=result[:, cols])
+            if (n, o) in partial:
+                nc.vector.tensor_tensor(out=result[:, t0:t1], in0=total, in1=partial[(n, o)][:, t0:t1], op=ALU.add)
+            else:
+                copy_out(result[:, t0:t1], total, on_vector=(o == 1))
+            nc.sync.dma_start(out=outs[o][n * P : (n + 1) * P, t0:t1], in_=result[:, t0:t1])
 
-        terms = ((("wi", "xn"), ("wr", "xr")), (("wr", "xi"), ("wi", "xr")))
-
+        round_on_both("xi", 0, 0)
+        negate_on_scalar(0, 0)
+        quantise("xi", 0, 0)
+        round_on_vector("xi", 0, HALF)
+        negate_on_scalar(0, HALF)
+        quantise("xn", 0, 0)
+        quantise("xi", 0, HALF)
+        quantise("xn", 0, HALF)
         for t0 in (0, HALF):
-            cast_vector("xi", 0, t0)
-            negate_scalar(0, t0)
-            quantise("xi", 0, t0)
-            quantise("xn", 0, t0)
-        for t0 in (0, HALF):
-            cast_shared("xr", 0, t0)
+            round_on_both("xr", 0, t0)
             quantise("xr", 0, t0)
 
         for t0 in (0, HALF):
             for n in FIRST:
-                mm("wr", "xi", 0, n, 1, t0, t0 + HALF, bank=2 * n + 1)
+                multiply_half(TERMS[1][0], 0, n, 1, t0, bank=2 * n + 1)
         for n in FIRST:
-            mm("wi", "xn", 0, n, 0, bank=2 * n)
+            multiply(TERMS[0][0], 0, n, 0, bank=2 * n)
+        for o in (0, 1):
+            for n in FIRST:
+                multiply_half(TERMS[o][1], 0, n, o, 0)
         for n in FIRST:
-            mm("wr", "xr", 0, n, 0, 0, HALF)
-        for n in FIRST:
-            mm("wr", "xr", 0, n, 0, HALF, T, stop=True)
-            park(n, 0)
-            mm("wi", "xr", 0, n, 1, stop=True)
-            park(n, 1, on_vector=True)
+            for o in (0, 1):
+                multiply_half(TERMS[o][1], 0, n, o, HALF, stop=True)
+                park(n, o, on_vector=(o == 1))
 
         for n in SECOND:
             for o in (0, 1):
-                mm(*terms[o][0], 0, n, o)
-                mm(*terms[o][1], 0, n, o, stop=True)
-                park(n, o)
+                multiply(TERMS[o][0], 0, n, o)
+                multiply(TERMS[o][1], 0, n, o, stop=True)
+                park(n, o, on_vector=(o == 1 and n % 2 == 0))
+
         for n in HELD:
             for o in (0, 1):
-                mm(*terms[o][0], 0, n, o)
-                mm(*terms[o][1], 0, n, o)
-
+                multiply(TERMS[o][0], 0, n, o)
+                multiply(TERMS[o][1], 0, n, o)
         for a in later:
-            final = a == PASSES - 1
-            cast_vector("xi", a, 0)
-            negate_vector(a)
+            last_pass = a == PASSES - 1
+            round_on_vector("xi", a, 0)
+            negate_on_scalar(a, 0)
             quantise("xi", a, 0)
             quantise("xn", a, 0)
-            cast_shared("xr", a, 0)
+            round_on_both("xr", a, 0)
             quantise("xr", a, 0)
             for o in (1, 0):
                 for n in HELD:
-                    mm(*terms[o][0], a, n, o)
+                    multiply(TERMS[o][0], a, n, o)
             for n in HELD:
                 for o in (0, 1):
-                    mm(*terms[o][1], a, n, o, stop=final)
-                    if final:
-                        finish(n, o, on_vector=(o == 1))
+                    multiply(TERMS[o][1], a, n, o, stop=last_pass)
+                    if last_pass:
+                        finish(n, o)
 
-        for n in range(FIRST.start, SECOND.stop):
+        for n in parked:
             for o in (0, 1):
-                steps = [(w, x, a) for a in later for (w, x) in terms[o]]
-                for s, (w, x, a) in enumerate(steps):
-                    mm(w, x, a, n, o, stop=(s == len(steps) - 1))
-                very_last = n == SECOND.stop - 1 and o == 1
-                finish(n, o, on_vector=(o == 1), pieces=2 if very_last else 1)
+                steps = [(term, a) for a in later for term in TERMS[o]]
+                if (n, o) == (parked.stop - 1, 1):
+                    for t0 in (0, HALF):
+                        for s, (term, a) in enumerate(steps):
+                            multiply_half(term, a, n, o, t0, stop=(s == len(steps) - 1))
+                        finish(n, o, t0, t0 + HALF)
+                else:
+                    for s, (term, a) in enumerate(steps):
+                        multiply(term, a, n, o, stop=(s == len(steps) - 1))
+                    finish(n, o)

from contextlib import ExitStack

import concourse.mybir as mybir

K, M, T = 1536, 1536, 512
FLOPS = 4 * 2 * K * M * T

F32 = mybir.dt.float32
BF16 = mybir.dt.bfloat16
I32 = mybir.dt.int32
U32 = mybir.dt.uint32
U8 = mybir.dt.uint8
FP8X4 = mybir.dt.float8_e4m3fn_x4
FP4X4 = mybir.dt.float4_e2m1fn_x4
ALU = mybir.AluOpType
ACT = mybir.ActivationFunctionType

P = 128
PACK = 4
K_PASS = P * PACK
PASSES = K // K_PASS
BANKS = 8
HALF = T // 2
QUARTER = T // 4
MX_ALIGN = 64
QUADRANT = 32
SCALE_ROWS = 4

FIRST_SCALE_ROW = {"wi": 0, "wr": SCALE_ROWS}
WORD_BYTES = {"wi": 2, "wr": 4}

FIRST = range(0, 4)
SECOND = range(4, 8)
HELD = range(8, 12)

TERMS = ((("wi", "xn"), ("wr", "xr")), (("wr", "xi"), ("wi", "xr")))

NEIGHBOURS = 2
VECTOR_EIGHTHS = 5
RESULT_BUFS = 10


def tile_mix_cplx_fm_none_kernel(tc, xr, xi, wr_words, wr_scales, wi_words, wi_scales, out_0, out_1):
    nc = tc.nc
    outs = (out_0, out_1)
    x_hbm = {"xr": xr, "xi": xi}
    words_hbm = {"wr": wr_words.rearrange("a p n j -> p a (n j)"), "wi": wi_words.rearrange("a p b -> p a b")}
    scales_hbm = {"wr": wr_scales, "wi": wi_scales}

    pass0, later = range(0, 1), range(1, PASSES)
    after_first, parked = range(SECOND.start, HELD.stop), range(FIRST.start, SECOND.stop)

    with ExitStack() as ctx:
        keep = ctx.enter_context(tc.tile_pool(name="keep", bufs=1))
        results = ctx.enter_context(tc.tile_pool(name="results", bufs=RESULT_BUFS))
        psum = ctx.enter_context(tc.psum_pool(name="psum", bufs=1))
        ctx.enter_context(tc.manual_schedule())

        raw = {}
        w_codes, w_scale = {}, {}

        def load_x(name, a, t0, t1):
            rows = keep.tile([P, PACK, t1 - t0], F32, name="raw_%s_%d_%d" % (name, a, t0))
            src = x_hbm[name][a * K_PASS : (a + 1) * K_PASS, t0:t1]
            nc.sync.dma_start(out=rows[:], in_=src.rearrange("(p j) w -> p j w", j=PACK))
            raw[(name, a, t0)] = rows

        def load_words(weight, passes, tiles):
            tile_bytes = P * WORD_BYTES[weight]
            words = keep.tile(
                [P, len(passes), len(tiles) * tile_bytes],
                U8,
                align_bytes=MX_ALIGN,
                name="words_%s_%d_%d" % (weight, passes.start, tiles.start),
            )
            src = words_hbm[weight][:, passes.start : passes.stop, tiles.start * tile_bytes : tiles.stop * tile_bytes]
            nc.sync.dma_start(out=words[:].bitcast(I32), in_=src.bitcast(I32))
            for a in passes:
                for n in tiles:
                    lo = (n - tiles.start) * tile_bytes
                    w_codes[(weight, a, n)] = words[:, a - passes.start, lo : lo + tile_bytes]

        def new_plane(name, passes, tiles):
            plane = keep.tile([P, len(passes), len(tiles) * P], U8, align_bytes=MX_ALIGN, name=name)
            nc.vector.memset(plane[:].bitcast(I32), 0)
            return plane

        def load_scales(plane, weight, passes, tiles):
            first_row = FIRST_SCALE_ROW[weight]
            src = scales_hbm[weight][passes.start : passes.stop, :, tiles.start * P : tiles.stop * P]
            src = src.rearrange("a (q r) n -> r q a n", r=SCALE_ROWS)
            for r in range(SCALE_ROWS):
                nc.sync.dma_start(out=plane[first_row + r : P : QUADRANT, :, :].bitcast(I32), in_=src[r].bitcast(I32))
            for a in passes:
                for n in tiles:
                    lo = (n - tiles.start) * P
                    w_scale[(weight, a, n)] = plane[first_row:, a - passes.start, lo : lo + P]

        plane_wr_first = new_plane("plane_wr_first", pass0, FIRST)
        plane_wi_first = new_plane("plane_wi_first", pass0, FIRST)
        plane_after_first = new_plane("plane_after_first", pass0, after_first)
        plane_held = new_plane("plane_held", later, HELD)
        plane_parked = new_plane("plane_parked", later, parked)

        load_x("xi", 0, 0, HALF)
        load_scales(plane_wr_first, "wr", pass0, FIRST)
        load_words("wr", pass0, FIRST)
        load_x("xi", 0, HALF, T)
        load_words("wi", pass0, FIRST)
        load_scales(plane_wi_first, "wi", pass0, FIRST)
        load_x("xr", 0, 0, HALF)
        load_x("xr", 0, HALF, T)
        load_scales(plane_after_first, "wi", pass0, after_first)
        load_words("wi", pass0, SECOND)
        load_words("wr", pass0, SECOND)
        load_scales(plane_after_first, "wr", pass0, after_first)
        load_words("wi", pass0, HELD)
        load_words("wr", pass0, HELD)
        for a in later:
            load_x("xi", a, 0, T)
            load_words("wr", range(a, a + 1), HELD)
            if a == later.start:
                load_scales(plane_held, "wr", later, HELD)
            load_words("wi", range(a, a + 1), HELD)
            load_x("xr", a, 0, T)
            if a == later.start:
                load_scales(plane_held, "wi", later, HELD)
        load_scales(plane_parked, "wi", later, parked)
        load_words("wi", later, FIRST)
        load_words("wr", later, FIRST)
        load_scales(plane_parked, "wr", later, parked)
        load_words("wi", later, SECOND)
        load_words("wr", later, SECOND)

        x_codes, x_scale = {}, {}
        for name in ("xr", "xi", "xn"):
            for a in range(PASSES):
                x_codes[(name, a)] = keep.tile([P, T], U32, align_bytes=MX_ALIGN, name="codes_%s_%d" % (name, a))
                x_scale[(name, a)] = keep.tile([P, T], U8, align_bytes=MX_ALIGN, name="scale_%s_%d" % (name, a))

        grouped = {}

        def new_grouped(name, source, a, t0):
            width = raw[(source, a, t0)].shape[2]
            grouped[(name, a, t0)] = keep.tile(
                [P, width, PACK], BF16, align_bytes=MX_ALIGN, name="grouped_%s_%d_%d" % (name, a, t0)
            )
            return width

        def interleave_views(name, source, a, t0, c0, c1):
            dst = grouped[(name, a, t0)][:, c0:c1, :].rearrange("p (c i) j -> p c j i", i=NEIGHBOURS)
            src = raw[(source, a, t0)][:, :, c0:c1].rearrange("p j (c i) -> p c j i", i=NEIGHBOURS)
            return dst, src

        def round_on_vector(name, a, t0):
            width = new_grouped(name, name, a, t0)
            dst, src = interleave_views(name, name, a, t0, 0, width)
            nc.vector.tensor_copy(out=dst, in_=src)

        def round_on_both(name, a, t0):
            width = new_grouped(name, name, a, t0)
            cut = width * VECTOR_EIGHTHS // 8
            dst, src = interleave_views(name, name, a, t0, 0, cut)
            nc.vector.tensor_copy(out=dst, in_=src)
            dst, src = interleave_views(name, name, a, t0, cut, width)
            nc.scalar.copy(out=dst, in_=src)

        def negate_on_scalar(a, t0):
            width = new_grouped("xn", "xi", a, t0)
            dst, src = interleave_views("xn", "xi", a, t0, 0, width)
            nc.scalar.activation(out=dst, in_=src, func=ACT.Copy, scale=-1.0)

        def quantise(name, a, t0):
            source = grouped[(name, a, t0)]
            t1 = t0 + source.shape[1]
            nc.vector.quantize_mx(
                out=x_codes[(name, a)][:, t0:t1].bitcast(FP8X4),
                scales=x_scale[(name, a)][:, t0:t1],
                in_=source[:].rearrange("p w j -> p (w j)"),
            )

        open_sums = {}
        partial = {}
        opened = []

        def multiply(term, a, n, o, t0=0, t1=T, stop=False, bank=None):
            weight, name = term
            start = (n, o) not in open_sums
            if start:
                if bank is None:
                    bank = len(opened) % BANKS
                opened.append((n, o))
                open_sums[(n, o)] = psum.tile([P, T], F32, name="bank%d" % bank)
            nc.tensor.matmul_mx(
                out=open_sums[(n, o)][:, t0:t1],
                lhsT=w_codes[(weight, a, n)].bitcast(FP8X4 if weight == "wr" else FP4X4),
                lhsT_scale=w_scale[(weight, a, n)],
                rhs=x_codes[(name, a)][:, t0:t1].bitcast(FP8X4),
                rhs_scale=x_scale[(name, a)][:, t0:t1],
                start=start,
                stop=stop,
            )

        def multiply_half(term, a, n, o, t0, stop=False, bank=None):
            width = HALF if term[0] == "wr" else QUARTER
            for lo in range(t0, t0 + HALF, width):
                multiply(term, a, n, o, lo, lo + width, stop=stop and lo + width == t0 + HALF, bank=bank)

        def copy_out(dst, src, on_vector):
            if on_vector:
                nc.vector.tensor_copy(out=dst, in_=src)
            else:
                nc.scalar.copy(out=dst, in_=src)

        def park(n, o, on_vector):
            partial[(n, o)] = keep.tile([P, T], F32, name="partial_%d_%d" % (n, o))
            copy_out(partial[(n, o)][:], open_sums.pop((n, o))[:], on_vector)

        def finish(n, o, t0=0, t1=T):
            total = open_sums.pop((n, o))[:, t0:t1]
            result = results.tile([P, T], F32, name="result")
            if (n, o) in partial:
                nc.vector.tensor_tensor(out=result[:, t0:t1], in0=total, in1=partial[(n, o)][:, t0:t1], op=ALU.add)
            else:
                copy_out(result[:, t0:t1], total, on_vector=(o == 1))
            nc.sync.dma_start(out=outs[o][n * P : (n + 1) * P, t0:t1], in_=result[:, t0:t1])

        round_on_both("xi", 0, 0)
        negate_on_scalar(0, 0)
        quantise("xi", 0, 0)
        round_on_vector("xi", 0, HALF)
        negate_on_scalar(0, HALF)
        quantise("xn", 0, 0)
        quantise("xi", 0, HALF)
        quantise("xn", 0, HALF)
        for t0 in (0, HALF):
            round_on_both("xr", 0, t0)
            quantise("xr", 0, t0)

        for t0 in (0, HALF):
            for n in FIRST:
                multiply_half(TERMS[1][0], 0, n, 1, t0, bank=2 * n + 1)
        for n in FIRST:
            multiply(TERMS[0][0], 0, n, 0, bank=2 * n)
        for o in (0, 1):
            for n in FIRST:
                multiply_half(TERMS[o][1], 0, n, o, 0)
        for n in FIRST:
            for o in (0, 1):
                multiply_half(TERMS[o][1], 0, n, o, HALF, stop=True)
                park(n, o, on_vector=(o == 1))

        for n in SECOND:
            for o in (0, 1):
                multiply(TERMS[o][0], 0, n, o)
                multiply(TERMS[o][1], 0, n, o, stop=True)
                park(n, o, on_vector=(o == 1 and n % 2 == 0))

        for n in HELD:
            for o in (0, 1):
                multiply(TERMS[o][0], 0, n, o)
                multiply(TERMS[o][1], 0, n, o)
        for a in later:
            last_pass = a == PASSES - 1
            round_on_vector("xi", a, 0)
            negate_on_scalar(a, 0)
            quantise("xi", a, 0)
            quantise("xn", a, 0)
            round_on_both("xr", a, 0)
            quantise("xr", a, 0)
            for o in (1, 0):
                for n in HELD:
                    multiply(TERMS[o][0], a, n, o)
            for n in HELD:
                for o in (0, 1):
                    multiply(TERMS[o][1], a, n, o, stop=last_pass)
                    if last_pass:
                        finish(n, o)

        for n in parked:
            for o in (0, 1):
                steps = [(term, a) for a in later for term in TERMS[o]]
                if (n, o) == (parked.stop - 1, 1):
                    for t0 in (0, HALF):
                        for s, (term, a) in enumerate(steps):
                            multiply_half(term, a, n, o, t0, stop=(s == len(steps) - 1))
                        finish(n, o, t0, t0 + HALF)
                else:
                    for s, (term, a) in enumerate(steps):
                        multiply(term, a, n, o, stop=(s == len(steps) - 1))
                    finish(n, o)
